import numpy as np, ml_dtypes
CORES = [6,15,38,47]
N = 4
import mx_ref
BF = ml_dtypes.bfloat16
def pick(q, e):
    c = np.concatenate([q[0].reshape(128, -1, 4), np.zeros((128, 1, 4), np.uint8)], axis=1); s = np.concatenate([q[1], np.ones((16, 1), np.uint8)], axis=1)
    return (np.ascontiguousarray(c[:, e].reshape(128, -1)), np.ascontiguousarray(s[:, e]))
def join(*qs):
    return (np.concatenate([q[0] for q in qs], axis=1), np.concatenate([q[1] for q in qs], axis=1))
def put(q, e, v):
    c, s = q[0].reshape(128, -1, 4).copy(), q[1].copy(); c[:, e] = v[0].reshape(128, -1, 4); s[:, e] = v[1]
    return (c.reshape(128, -1), s)
def pk(c, s):
    return (np.ascontiguousarray(c), mx_ref.live(s))
def emit(q):
    return q[0], q[1]
def cut(t, i, w=512):
    return t[:, w * i:w * i + w]
def f(rng, *shape):
    return mx_ref.flush((rng.standard_normal(shape, dtype=np.float32) * np.exp2(rng.integers(-2, 3, shape[:-1] + (1,)))).astype(BF))
def wide(rng, *shape, cols=0):
    v = rng.standard_normal(shape, dtype=np.float32) * np.exp2(rng.integers(-12, 13, shape)).astype(np.float32)
    if cols: v *= np.repeat(np.exp2(rng.integers(-cols, cols + 1, shape[:-2] + (1, shape[-1] // 4))) * (rng.random(shape[:-2] + (1, shape[-1] // 4)) > 0.0625), 4, axis=-1).astype(np.float32)
    return mx_ref.flush(v.astype(BF))
P, R, O = 1024, 5, 2
C = P // 16
CLOUD = np.arange(N * P) % P // C
def same(t):
    return np.stack([t] * N)
def sizes(rng, *shape):
    return (1 + rng.random(shape, dtype=np.float32)) * (1 - 2 * rng.integers(0, 2, shape)).astype(np.float32)
def setup_inputs(rng):
    return {"x": f(rng, N, 128, 4 * P), "seed": same(f(rng, 128, 64)), "w": f(rng, N, 128, 512 * O)}
def setup_inputs_again(rng):
    d = setup_inputs(rng)
    half = rng.permutation(16) < 8
    four = rng.permutation(np.flatnonzero(half))[:4]
    huge, minus = np.isin(np.arange(16), four), np.isin(np.arange(16), four[:2])
    x, s = sizes(rng, N, 128, 4 * P), sizes(rng, 128, 64)
    x = np.where(np.repeat(half, 4 * C), np.abs(x), x)
    s = np.where(np.repeat(half, 4), np.abs(s), s)
    for b in np.flatnonzero(half):
        r, j = int(rng.integers(0, N)), int(b * C + rng.integers(0, C))
        if minus[b]: r, j = 0, int(b * C)
        x[r, :, 4 * j:4 * j + 4] *= np.float32(0.5 if huge[b] else 2.0 ** -8)
    by = np.where(huge, np.float32(2.0 ** 29), np.float32(1))
    x, s = x * np.repeat(by, 4 * C), s * np.repeat(np.where(minus, -by, by), 4)
    d["x"], d["seed"] = x.astype(BF), same(s.astype(BF))
    return d
def setup_inputs_late(rng):
    d = setup_inputs(rng)
    top = (np.arange(128) < 64)[:, None]
    a = np.stack([rng.permutation(C) < C // 2 for i in range(16 * N)]).reshape(N, 1, P)
    a = np.repeat(a, 4, axis=2)
    v = sizes(rng, N, 128, 4 * P)
    d["x"] = np.where(top, np.where(a, -np.abs(v), v * np.float32(2.0 ** -6)), np.where(a, 0, v)).astype(BF)
    d["seed"] = same(np.where(top, np.abs(sizes(rng, 128, 64)), 0).astype(BF))
    return d
def setup_inputs_one(rng):
    d = setup_inputs(rng)
    h = int(rng.integers(0, N))
    s = sizes(rng, 128, 64).astype(BF)
    d["seed"] = same(s)
    d["x"] = same(np.repeat(s.reshape(128, 16, 1, 4), C, axis=2).reshape(128, 4 * P))
    d["x"][h] = (sizes(rng, 128, 4 * P) * np.float32(2.0 ** -6)).astype(BF)
    return d
def setup_inputs_spread(rng):
    d = setup_inputs(rng)
    x, s = wide(rng, N, 128, 4 * P, cols=6).astype(np.float32), wide(rng, 128, 64).astype(np.float32)
    plus = rng.permutation(16) < 4
    x = np.where(np.repeat(plus, 4 * C), np.abs(x), x)
    s = np.where(np.repeat(plus, 4), np.abs(s), s)
    for b in np.flatnonzero(plus):
        for r, zero in zip(np.sort(rng.permutation(N)[:2]), (0.0, -0.0)):
            j = int(b * C + rng.integers(0, C))
            x[r, :, 4 * j:4 * j + 4] = np.float32(zero)
    d["x"], d["seed"] = x.astype(BF), same(s.astype(BF))
    return d
def setup_inputs_ties(rng):
    d = setup_inputs(rng)
    v = rng.standard_normal((128, 16, 12, 4), dtype=np.float32)
    v[:64, 1::2, 1::2] = v[:64, 1::2, ::2]
    s = rng.standard_normal((128, 16, 4), dtype=np.float32)
    s[64:, 1::2] = 0
    x = np.zeros((N, 128, 16, C, 4), np.float32)
    for b in range(16):
        own = np.stack([rng.permutation(N) < N // 2 for i in range(12)])
        own[1] = ~own[0]
        for r in range(N):
            e = rng.permutation(np.resize(np.flatnonzero(own[:, r]), C))
            x[r][:, b] = v[:, b][:, e]
    d["x"] = mx_ref.flush(x.reshape(N, 128, 4 * P).astype(BF))
    d["seed"] = same(mx_ref.flush(s.reshape(128, 64).astype(BF)))
    return d
def check_inputs(d):
    b = []
    for k in ("x", "seed", "w"):
        v = np.abs(d[k].astype(np.float32))
        if not (np.isfinite(v).all() and ((v == 0) | (v >= 2.0 ** -30) & (v <= 2.0 ** 30)).all()): b.append("a value of " + k)
    s = d["seed"].astype(np.float32)
    if not (s == s[:1]).all(): b.append("seed isn't the same on all ranks")
    return b
def reference(x, seed, w):
    q = [mx_ref.quantize(np.ascontiguousarray(x[r])) for r in range(N)]
    every = join(*q)
    c = mx_ref.quantize(np.ascontiguousarray(seed[0]))
    won, nb = [], np.zeros((R, 16), np.float32)
    for t in range(R):
        k = pick(c, np.concatenate([np.arange(16), np.full(112, -1)]))
        s = np.concatenate([mx_ref.matmul(k, v)[:16] for v in q], axis=1)
        s = s[CLOUD, np.arange(N * P)] + np.float32(0)
        m = s if t == 0 else np.maximum(m, s)
        e = []
        for b in range(16):
            i = np.flatnonzero(CLOUD == b)
            e.append(int(i[np.argmin(m[i])]))
        c = pick(every, np.array(e))
        won.append(c)
        nb[t] = e
    u = join(*won)
    oc, osc = emit(u)
    y = np.stack([np.concatenate([mx_ref.matmul(mx_ref.quantize(np.ascontiguousarray(cut(w[r], o))), u) for o in range(O)], axis=1) for r in range(N)])
    return {"oc": same(oc), "osc": same(osc), "nb": same(nb), "y": y}

@@ -1,0 +1,268 @@
+from concourse.mybir import dt, AluOpType, ActivationFunctionType
+
+N, P, R, O = 4, 1024, 5, 2
+B = 16
+C = P // B
+BIG = 2.0 ** 98
+F8, U8, F32, BF, I32, U16 = "float8_e4m3fn_x4", "uint8", "float32", "bfloat16", "int32", "uint16"
+CHUNKS = [(0, 256), (256, 640), (640, 896), (896, 1024)]
+
+SCRATCH = {
+    "xt": ("sbuf", [128, 4 * P], BF), "xq": ("sbuf", [128, P], F8), "xs": ("sbuf", [128, P], U8),
+    "st": ("sbuf", [128, 512], BF),
+    "wt": ("sbuf", [128, 512 * O], BF), "wq": ("sbuf", [128, 128 * O], F8), "ws": ("sbuf", [128, 128 * O], U8),
+    "sq": ("sbuf", [128, 128], F8), "ss": ("sbuf", [128, 128], U8),
+    "aq": ("sbuf", [128, 192], F8), "as_": ("sbuf", [128, 192], U8),
+    "bq": ("sbuf", [128, 192], F8), "bs": ("sbuf", [128, 192], U8),
+    "hq": ("sbuf", [128, 128], F8), "hs": ("sbuf", [128, 128], U8),
+    "e": ("sbuf", [128, 32], F32), "f": ("sbuf", [128, 64], F32), "r": ("sbuf", [128, 64 * R], F32),
+    "junk": ("sbuf", [128, 64], F32), "ni": ("sbuf", [128, 8], F32),
+    "rx1": ("sbuf", [128, 8], F32), "tx2": ("sbuf", [128, 8], F32), "rx2": ("sbuf", [128, 8], F32),
+    "sel": ("sbuf", [128, 16], F32), "dd": ("sbuf", [128, 16], F32), "n1": ("sbuf", [128, 8], F32),
+    "off": ("sbuf", [128, 64], U16),
+    "ip": ("sbuf", [128, 4], I32),
+    "bb": ("sbuf", [128, 4], F32),
+    "nn": ("sbuf", [128, 32], F32), "nt": ("sbuf", [128, 32], F32),
+    "yo": ("sbuf", [128, 80 * O], F32), "yl": ("sbuf", [128, B * O], F32),
+    "ps": ("psum", [128, 4096], F32),
+}
+_LOCAL = ["sz", "zf", "zr", "io1", "k1", "k2", "k3", "seed", "sq", "w", "wq", "x0", "x1", "x2", "x3", "zq",
+          "xq", "pe", "exa", "tr", "scan", "sgn", "num", "lst", "pkc", "pks",
+          "w1", "sela", "la", "t2", "n2", "da", "pac", "pas", "selb", "lb", "db", "nn", "pbc", "pbs",
+          "ws2", "pw", "py0", "py1", "yv", "yl0", "yl1", "ntr", "dsy", "dsc", "sent"]
+_ARRIVE = ["%s%d_%d" % (k, h, t) for k in "csm" for h in (1, 2) for t in range(1, R + 1)]
+SEMAPHORES = _LOCAL + _ARRIVE
+
+
+def rank_program(g, core, T, topo):
+    rank = T.rank_of(core)
+    if rank is None:
+        return
+    V, S, PE, SY = g.vector, g.scalar, g.tensor, g.sync
+    A, AF = AluOpType, ActivationFunctionType
+    tot, seen = {}, {}
+
+    def inc(ins, s, n=1):
+        ins.then_inc(T.sem[s], n)
+        tot[s] = tot.get(s, 0) + n
+
+    def w(q, name, *sems):
+        for s in sems:
+            if seen.get((name, s), 0) < tot[s]:
+                q.wait_ge(T.sem[s], tot[s])
+                seen[(name, s)] = tot[s]
+                seen[s] = max(seen.get(s, 0), tot[s])
+
+    def wv(*s): w(V, "v", *s)
+    def wsc(*s): w(S, "s", *s)
+    def wp(*s): w(PE, "p", *s)
+    def wg(*s): w(g, "g", *s)
+    def wy(*s): w(SY, "y", *s)
+
+    def cds(name, a, b): return T[name][:, a:b].bitcast(dt.uint8)
+    def wds(name, a, b): return T[name][:, a:b].bitcast(dt.uint32)
+    def lst(i): return T.off[:, 2 * i:2 * i + 1]
+
+    def send(peer, dst, src, arrive):
+        rid, pid, _ = topo.addr(peer)
+        g.remote_dma(dst, src, T.sem[arrive], T.sem.sent, pid, rid, topo.mask(core, peer))
+        tot["sent"] = tot.get("sent", 0) + len(topo.engines(core, peer))
+
+    mate = T.cores[rank ^ 1]
+    cross = T.cores[rank ^ 2]
+    arrive_mate = len(topo.engines(mate, core))
+    arrive_cross = len(topo.engines(cross, core))
+
+    inc(S.dma_start(T.st[:, 0:64], T.seed[:]), "seed", 16)
+    for i, (a, b) in enumerate(CHUNKS):
+        q = (SY, S)[i % 2]
+        inc(q.dma_start(T.xt[:, 4 * a:4 * b], T.x[:, 4 * a:4 * b]), "x%d" % i, 16)
+    inc(S.dma_start(T.wt[:], T.w[:]), "w", 16)
+
+    inc(g.iota(T.ip[:, 0:1], [[0, 1]], 0, 1), "io1")
+    inc(V.memset(T.st[:, 64:512], 0.0), "sz")
+    inc(V.memset(T.r[64:128, C - 1:C], 0.0), "zr")
+    wv("io1")
+    inc(V.tensor_scalar(T.ip[:, 2:3], T.ip[:, 0:1], B - 1, None, A.bitwise_and), "k1")
+    wv("k1")
+    inc(V.tensor_copy(T.bb[:, 0:1], T.ip[:, 2:3]), "k2")
+    wv("k2")
+    inc(V.tensor_scalar(T.bb[:, 1:2], T.bb[:, 0:1], float(C), None, A.mult), "k3")
+    inc(V.tensor_scalar(T.bb[:, 2:3], T.bb[:, 0:1], float(C), float(P * rank), A.mult, A.add), "k3")
+    wv("seed", "sz", "k3")
+    inc(V.quantize_mx(T.sq[:], T.ss[:], T.st[:]), "sq")
+
+    def score(k, mq, ms):
+        inc(PE.matmul_mx(T.ps[:, 512 * k:512 * k + 128], T.xq[:, 128 * k:128 * k + 128], T.xs[:, 128 * k:128 * k + 128],
+                         T[mq][:, 0:128], T[ms][:, 0:128], True, True), "pe")
+
+    def mark(t): return slice(C * t - 1, C * t)
+
+    def local(t, at):
+        co = max(0, B * (t - 2))
+        wv("pe", *(["tr"] if t > 1 else []))
+        for h in (0, B):
+            for a in (0, 1):
+                src = T.ps[64 * a:64 * a + 64, co + a:co + a + 514 * 7 + 1:514]
+                dst = T.e[0:64, h + a:h + B:2]
+                inc(V.tensor_copy(dst, src) if t == 1 else V.tensor_tensor(dst, src, dst, A.max), "exa")
+        wv("exa")
+        for o in (0, 32):
+            for h in (0, 32):
+                inc(V.transpose(T.f[o:o + 32, h:h + 32], T.e[h:h + 32, 0:32]), "tr")
+        run = T.r[0:64, C * (t - 1):C * t]
+        ni = T.ni[0:64, t:t + 1]
+        wv("tr")
+        inc(V.tensor_tensor_scan(run, T.f[0:64, :], T.f[0:64, :], BIG, A.min, A.min), "scan")
+        wsc("scan")
+        inc(S.activation(T.junk[0:64, :], run, AF.Sign, bias=T.r[0:64, mark(t)], scale=-1.0, accum_out=ni), "sgn")
+        wv("sgn")
+        for p in (0, 64):
+            inc(V.tensor_scalar(T.off[p:p + 64, 2 * t:2 * t + 1], ni, -1.0, T.bb[0:64, 1:2], A.mult, A.add), "lst")
+        wsc("sgn", "k3")
+        if t == R:
+            inc(S.activation(T.r[96:128, mark(t)], T.ni[0:32, t:t + 1], AF.Identity, bias=T.bb[0:32, 2:3], scale=-1.0), "num")
+        wv("lst", "xq")
+        inc(V.tensor_copy(wds("aq", at, at + B), wds("xq", 0, P).indirect(lst(t))), "pkc")
+        wsc("lst", "xq")
+        inc(S.activation(T.as_[:, at:at + B], T.xs[:, 0:P].indirect(lst(t)), AF.Copy), "pks")
+        if t < R:
+            inc(S.activation(T.n1[64:128, t:t + 1], ni, AF.Identity, bias=T.bb[0:64, 2:3], scale=-1.0), "num")
+
+    n = B * R
+    n0 = n - B
+    for t in range(1, R + 1):
+        last = t == R
+        c0 = 32 * (t - 1)
+        col = slice(t, t + 1)
+        sc = slice(8 + t, 9 + t)
+        mk = mark(t)
+        up = slice(64, 96 if last else 128)
+        sums = "w1" if t > 1 else "zr"
+        if t == 1:
+            wp("sq")
+            for i, (a, b) in enumerate(CHUNKS):
+                wv("x%d" % i)
+                inc(V.quantize_mx(T.xq[:, a:b], T.xs[:, a:b], T.xt[:, 4 * a:4 * b]), "xq")
+                wp("xq")
+                for k in range(a // 128, b // 128):
+                    score(k, "sq", "ss")
+        else:
+            wp("pbc", "pbs", "zq")
+            for k in range(8):
+                score(k, "hq", "hs")
+        local(t, c0)
+
+        wg("scan", sums, *(["num"] if last else []))
+        send(mate, T.rx1[:, col], T.r[:, mk], "m1_%d" % t)
+        wg("pkc")
+        send(mate, cds("aq", c0 + B, c0 + 2 * B), cds("aq", c0, c0 + B), "c1_%d" % t)
+        wg("pks")
+        send(mate, T.as_[:, c0 + B:c0 + 2 * B], T.as_[:, c0:c0 + B], "s1_%d" % t)
+
+        if t == 1:
+            inc(V.quantize_mx(T.hq[:], T.hs[:], T.st[:]), "zq")
+            inc(V.memset(T.nn[:], 0.0), "zf")
+        if t == 2:
+            wv("w")
+            inc(V.quantize_mx(T.wq[:], T.ws[:], T.wt[:]), "wq")
+        if last:
+            wp("wq", "exa")
+            for o in range(O):
+                inc(PE.matmul_mx(T.ps[:, 512 * o:512 * o + 128], T.wq[:, 128 * o:128 * o + 128],
+                                 T.ws[:, 128 * o:128 * o + 128], T.hq[:], T.hs[:], True, True), "pw")
+            wv("pw")
+            for o in range(O):
+                inc(V.tensor_copy(T.yo[:, n * o:n * o + n0], T.ps[:, 512 * o:512 * o + n0]), "yv")
+            wy("pbc", "pbs")
+            inc(SY.dma_start(T.oc[:, 0:4 * n0], cds("hq", 0, n0)), "dsy", 16)
+            for k in range(4):
+                inc(SY.dma_start(T.osc[4 * k:4 * k + 4, 0:n0], T.hs[32 * k:32 * k + 4, 0:n0]), "dsy", 16)
+            wy("yv")
+            for o in range(O):
+                inc(SY.dma_start(T.y[:, n * o:n * o + n0], T.yo[:, n * o:n * o + n0]), "dsy", 16)
+
+        V.wait_ge(T.sem["m1_%d" % t], arrive_mate)
+        less = A.is_lt if rank & 1 == 0 else A.is_le
+        inc(V.tensor_scalar(T.sel[64:128, col], T.rx1[0:64, col], T.r[0:64, mk], None, less), "sela")
+        inc(V.tensor_scalar(T.sel[0:64, col], T.rx1[0:64, col], T.r[0:64, mk], None, less), "sela")
+        inc(V.tensor_tensor(T.tx2[0:64, col], T.rx1[0:64, col], T.r[0:64, mk], A.min), "t2")
+        wv("sela")
+        inc(V.tensor_scalar(lst(8 + t), T.sel[:, col], float(B), T.bb[:, 0:1], A.mult, A.add), "la")
+        wsc("num", sums)
+        S.wait_ge(T.sem["m1_%d" % t], arrive_mate)
+        if last:
+            inc(S.activation(T.dd[96:128, col], T.r[96:128, mk], AF.Identity, bias=T.rx1[96:128, col], scale=-1.0), "da")
+        inc(S.activation(T.tx2[up, col], T.rx1[up, col], AF.Identity, bias=T.r[up, mk]), "n2")
+        if last:
+            wsc("da", "sela")
+            inc(S.activation(T.tx2[96:128, col], T.dd[96:128, col], AF.Identity, bias=T.r[96:128, mk],
+                             scale=T.sel[96:128, col]), "n2")
+        wg("t2", "n2")
+        send(cross, T.rx2[:, col], T.tx2[:, col], "m2_%d" % t)
+        wv("la", "pkc")
+        V.wait_ge(T.sem["c1_%d" % t], arrive_mate)
+        inc(V.tensor_copy(wds("bq", c0, c0 + B), wds("aq", c0, c0 + 2 * B).indirect(lst(8 + t))), "pac")
+        wv("pks")
+        V.wait_ge(T.sem["s1_%d" % t], arrive_mate)
+        inc(V.tensor_copy(T.bs[:, c0:c0 + B], T.as_[:, c0:c0 + 2 * B].indirect(lst(8 + t))), "pas")
+
+        wg("pac")
+        send(cross, cds("bq", c0 + B, c0 + 2 * B), cds("bq", c0, c0 + B), "c2_%d" % t)
+        wg("pas")
+        send(cross, T.bs[:, c0 + B:c0 + 2 * B], T.bs[:, c0:c0 + B], "s2_%d" % t)
+
+        wv("t2")
+        V.wait_ge(T.sem["m2_%d" % t], arrive_cross)
+        less = A.is_lt if rank & 2 == 0 else A.is_le
+        inc(V.tensor_scalar(T.sel[0:64, sc], T.rx2[0:64, col], T.tx2[0:64, col], None, less), "selb")
+        inc(V.tensor_scalar(T.sel[64:128, sc], T.rx2[0:64, col], T.tx2[0:64, col], None, less), "selb")
+        wv("selb")
+        inc(V.tensor_scalar(lst(16 + t), T.sel[:, sc], float(B), T.bb[:, 0:1], A.mult, A.add), "lb")
+        if t > 1:
+            wsc("n2", "zf")
+            S.wait_ge(T.sem["m2_%d" % t], arrive_cross)
+            if last:
+                inc(S.activation(T.dd[96:128, sc], T.tx2[96:128, col], AF.Identity, bias=T.rx2[96:128, col], scale=-1.0), "db")
+            inc(S.activation(T.nn[96:128, t - 2:t - 1], T.rx2[64:96, col], AF.Identity, bias=T.tx2[64:96, col]), "nn")
+            if last:
+                wsc("db", "selb")
+                inc(S.activation(T.nn[96:128, t - 1:t], T.dd[96:128, sc], AF.Identity, bias=T.tx2[96:128, col],
+                                 scale=T.sel[96:128, sc]), "nn")
+        h0 = B * (t - 1)
+        wv("lb", "pac", "zq")
+        V.wait_ge(T.sem["c2_%d" % t], arrive_cross)
+        inc(V.tensor_copy(wds("hq", h0, h0 + B), wds("bq", c0, c0 + 2 * B).indirect(lst(16 + t))), "pbc")
+        wv("pas")
+        V.wait_ge(T.sem["s2_%d" % t], arrive_cross)
+        inc(V.tensor_copy(T.hs[:, h0:h0 + B], T.bs[:, c0:c0 + 2 * B].indirect(lst(16 + t))), "pbs")
+        if not last:
+            inc(V.tensor_tensor(T.dd[64:128, sc], T.sel[64:128, col], T.sel[64:128, sc], A.add), "ws2")
+            wv("ws2", "num")
+            nxt = slice(64, 96 if t + 1 == R else 128)
+            inc(V.tensor_scalar(T.r[nxt, mark(t + 1)], T.dd[nxt, sc], 0.0, T.n1[nxt, col], A.is_equal, A.mult), "w1")
+
+    wp("pbc", "pbs")
+    for o in range(O):
+        inc(PE.matmul_mx(T.ps[:, 1024 + 512 * o:1024 + 512 * o + 128], T.wq[:, 128 * o:128 * o + 128],
+                         T.ws[:, 128 * o:128 * o + 128], T.hq[:], T.hs[:], True, True), "py%d" % o)
+    wy("pbc")
+    inc(SY.dma_start(T.oc[:, 4 * n0:4 * n], cds("hq", n0, n)), "dsy", 16)
+    wsc("pbs")
+    for k in range(4):
+        inc(S.dma_start(T.osc[4 * k:4 * k + 4, n0:n], T.hs[32 * k:32 * k + 4, n0:n]), "dsc", 16)
+    wv("nn")
+    inc(V.transpose(T.nt[96:128, :], T.nn[96:128, :]), "ntr")
+    wy("ntr")
+    inc(SY.dma_start(T.nb[:], T.nt[96:96 + R, 0:B]), "dsy", 16)
+    wv("py0")
+    inc(V.tensor_copy(T.yl[:, 0:B], T.ps[:, 1024 + n0:1024 + n]), "yl0")
+    wsc("py1")
+    inc(S.activation(T.yl[:, B:2 * B], T.ps[:, 1536 + n0:1536 + n], AF.Copy), "yl1")
+    wy("yl0")
+    inc(SY.dma_start(T.y[:, n0:n], T.yl[:, 0:B]), "dsy", 16)
+    wsc("yl1")
+    inc(S.dma_start(T.y[:, n + n0:2 * n], T.yl[:, B:2 * B]), "dsc", 16)
+    for s in tot:
+        if seen.get(s, 0) < tot[s]:
+            wg(s)

@@ -6,30 +6,38 @@ C = P // B
 BIG = 2.0 ** 98
 F8, U8, F32, BF, I32, U16 = "float8_e4m3fn_x4", "uint8", "float32", "bfloat16", "int32", "uint16"
 CHUNKS = [(0, 256), (256, 640), (640, 896), (896, 1024)]
+Z = 128
+GAP = B + Z
+WB = Z + 2 * GAP * (R - 1) + 2 * B
 
 SCRATCH = {
     "xt": ("sbuf", [128, 4 * P], BF), "xq": ("sbuf", [128, P], F8), "xs": ("sbuf", [128, P], U8),
-    "st": ("sbuf", [128, 512], BF),
+    "st": ("sbuf", [128, 576], BF),
     "wt": ("sbuf", [128, 512 * O], BF), "wq": ("sbuf", [128, 128 * O], F8), "ws": ("sbuf", [128, 128 * O], U8),
     "sq": ("sbuf", [128, 128], F8), "ss": ("sbuf", [128, 128], U8),
     "aq": ("sbuf", [128, 192], F8), "as_": ("sbuf", [128, 192], U8),
-    "bq": ("sbuf", [128, 192], F8), "bs": ("sbuf", [128, 192], U8),
+    "bq": ("sbuf", [128, WB], F8), "bs": ("sbuf", [128, WB], U8),
     "hq": ("sbuf", [128, 128], F8), "hs": ("sbuf", [128, 128], U8),
-    "e": ("sbuf", [128, 32], F32), "f": ("sbuf", [128, 64], F32), "r": ("sbuf", [128, 64 * R], F32),
-    "junk": ("sbuf", [128, 64], F32), "ni": ("sbuf", [128, 8], F32),
+    "e": ("sbuf", [128, 32], F32), "ea": ("sbuf", [128, 32], F32), "eb": ("sbuf", [128, 32], F32),
+    "f": ("sbuf", [128, 64], F32), "fa": ("sbuf", [128, 64], F32), "dm": ("sbuf", [128, 64], F32),
+    "g1": ("sbuf", [128, 64], F32), "g2": ("sbuf", [128, 64], F32), "g3": ("sbuf", [128, 64], F32),
+    "r": ("sbuf", [128, 64 * R], F32), "ra": ("sbuf", [128, 64 * R], F32),
+    "junk": ("sbuf", [128, 64], F32), "ni": ("sbuf", [128, 8], F32), "nia": ("sbuf", [128, 8], F32),
+    "sp": ("sbuf", [128, 16 * R], F32), "kk": ("sbuf", [128, 2], F32),
     "rx1": ("sbuf", [128, 8], F32), "tx2": ("sbuf", [128, 8], F32), "rx2": ("sbuf", [128, 8], F32),
     "sel": ("sbuf", [128, 16], F32), "dd": ("sbuf", [128, 16], F32), "n1": ("sbuf", [128, 8], F32),
     "off": ("sbuf", [128, 64], U16),
-    "ip": ("sbuf", [128, 4], I32),
-    "bb": ("sbuf", [128, 4], F32),
+    "ip": ("sbuf", [128, 4], I32), "ia": ("sbuf", [128, 8], F32),
+    "bb": ("sbuf", [128, 12], F32),
     "nn": ("sbuf", [128, 32], F32), "nt": ("sbuf", [128, 32], F32),
     "yo": ("sbuf", [128, 80 * O], F32), "yl": ("sbuf", [128, B * O], F32),
     "ps": ("psum", [128, 4096], F32),
 }
-_LOCAL = ["sz", "zf", "zr", "io1", "k1", "k2", "k3", "seed", "sq", "w", "wq", "x0", "x1", "x2", "x3", "zq",
+_LOCAL = ["sz", "zf", "zr", "io1", "io2", "k1", "k2", "k3", "seed", "sq", "w", "wq", "x0", "x1", "x2", "x3", "zq",
           "xq", "pe", "exa", "tr", "scan", "sgn", "num", "lst", "pkc", "pks",
-          "w1", "sela", "la", "t2", "n2", "da", "pac", "pas", "selb", "lb", "db", "nn", "pbc", "pbs",
-          "ws2", "pw", "py0", "py1", "yv", "yl0", "yl1", "ntr", "dsy", "dsc", "sent"]
+          "pea", "exb", "tra", "scana", "sgna", "fac", "pre", "prep", "ns1", "xn", "gs", "ga", "te",
+          "sela", "la", "t2", "n2", "da", "pac", "pas", "selb", "lb", "db", "nn", "pbc", "pbs", "pbt",
+          "pw", "py0", "py1", "yv", "yl0", "yl1", "ntr", "dsy", "dsc", "sent"]
 _ARRIVE = ["%s%d_%d" % (k, h, t) for k in "csm" for h in (1, 2) for t in range(1, R + 1)]
 SEMAPHORES = _LOCAL + _ARRIVE
 
@@ -48,7 +56,7 @@ def rank_program(g, core, T, topo):
 
     def w(q, name, *sems):
         for s in sems:
-            if seen.get((name, s), 0) < tot[s]:
+            if seen.get((name, s), 0) < tot.get(s, 0):
                 q.wait_ge(T.sem[s], tot[s])
                 seen[(name, s)] = tot[s]
                 seen[s] = max(seen.get(s, 0), tot[s])
@@ -61,7 +69,7 @@ def rank_program(g, core, T, topo):
 
     def cds(name, a, b): return T[name][:, a:b].bitcast(dt.uint8)
     def wds(name, a, b): return T[name][:, a:b].bitcast(dt.uint32)
-    def lst(i): return T.off[:, 2 * i:2 * i + 1]
+    def lst(i, k=1): return T.off[:, 2 * i:2 * i + k]
 
     def send(peer, dst, src, arrive):
         rid, pid, _ = topo.addr(peer)
@@ -73,6 +81,16 @@ def rank_program(g, core, T, topo):
     arrive_mate = len(topo.engines(mate, core))
     arrive_cross = len(topo.engines(cross, core))
 
+    def at_a(t): return Z + 2 * GAP * (t - 1)
+    def at_b(t): return at_a(t) + (GAP if t < R else B)
+
+    def zeros(*cols):
+        for c in cols:
+            inc(V.quantize_mx(T.bq[:, c:c + Z], T.bs[:, c:c + Z], T.st[:, 64:576]), "zq")
+
+    lo, hi, al = slice(0, 64), slice(64, 128), slice(0, 128)
+    q0, q1, up, top = slice(0, 32), slice(32, 64), slice(64, 96), slice(96, 128)
+
     inc(S.dma_start(T.st[:, 0:64], T.seed[:]), "seed", 16)
     for i, (a, b) in enumerate(CHUNKS):
         q = (SY, S)[i % 2]
@@ -80,65 +98,102 @@ def rank_program(g, core, T, topo):
     inc(S.dma_start(T.wt[:], T.w[:]), "w", 16)
 
     inc(g.iota(T.ip[:, 0:1], [[0, 1]], 0, 1), "io1")
-    inc(V.memset(T.st[:, 64:512], 0.0), "sz")
-    inc(V.memset(T.r[64:128, C - 1:C], 0.0), "zr")
+    inc(g.iota(T.ia[:, 0:R - 1], [[2 * GAP, R - 1]], Z, 0, allow_small_or_imprecise_dtypes=True), "io2")
+    inc(V.memset(T.st[:, 64:576], 0.0), "sz")
+    inc(V.memset(T.r[hi, C - 1:C * R:C], 0.0), "zr")
+    inc(V.memset(T.tx2[top, :], 0.0), "zr")
     wv("io1")
     inc(V.tensor_scalar(T.ip[:, 2:3], T.ip[:, 0:1], B - 1, None, A.bitwise_and), "k1")
+    inc(V.memset(T.nn[:], 0.0), "zf")
     wv("k1")
     inc(V.tensor_copy(T.bb[:, 0:1], T.ip[:, 2:3]), "k2")
-    wv("k2")
+    inc(V.memset(T.dm[lo, :], -BIG), "zf")
+    wv("k2", "io2")
     inc(V.tensor_scalar(T.bb[:, 1:2], T.bb[:, 0:1], float(C), None, A.mult), "k3")
     inc(V.tensor_scalar(T.bb[:, 2:3], T.bb[:, 0:1], float(C), float(P * rank), A.mult, A.add), "k3")
-    wv("seed", "sz", "k3")
-    inc(V.quantize_mx(T.sq[:], T.ss[:], T.st[:]), "sq")
+    inc(V.tensor_scalar(T.bb[:, 4:3 + R], T.ia[:, 0:R - 1], T.bb[:, 0:1], None, A.add), "k3")
+    inc(V.memset(T.kk[lo, 0:1], -1.0), "zf")
+    inc(V.memset(T.kk[lo, 1:2], -BIG), "zf")
+    wv("sz")
+    zeros(0, at_a(1) + B)
+    wv("seed", "k3")
+    inc(V.quantize_mx(T.sq[:], T.ss[:], T.st[:, 0:512]), "sq")
 
-    def score(k, mq, ms):
-        inc(PE.matmul_mx(T.ps[:, 512 * k:512 * k + 128], T.xq[:, 128 * k:128 * k + 128], T.xs[:, 128 * k:128 * k + 128],
-                         T[mq][:, 0:128], T[ms][:, 0:128], True, True), "pe")
+    def product(bank, k, mq, ms, c, first, final, sem):
+        inc(PE.matmul_mx(T.ps[:, 512 * bank:512 * bank + 128], T.xq[:, 128 * k:128 * k + 128], T.xs[:, 128 * k:128 * k + 128],
+                         T[mq][:, c:c + 128], T[ms][:, c:c + 128], first, final), sem)
+
+    def scores(bank, c, sem):
+        for k in range(8):
+            product(bank, k, "bq", "bs", c - B * k, k == 0, k == 7, sem)
 
     def mark(t): return slice(C * t - 1, C * t)
+    def msg(rows, t): return T.r[rows, mark(t)]
+    def sp(rows, t, i, k=1): return T.sp[rows, 16 * t + i:16 * t + i + k]
+    NS, NEG, NB, NNS, INIT, B1, B2, X1, NS1 = range(9)
 
-    def local(t, at):
-        co = max(0, B * (t - 2))
-        wv("pe", *(["tr"] if t > 1 else []))
+    def fold(to, co, step, sem):
         for h in (0, B):
             for a in (0, 1):
-                src = T.ps[64 * a:64 * a + 64, co + a:co + a + 514 * 7 + 1:514]
-                dst = T.e[0:64, h + a:h + B:2]
-                inc(V.tensor_copy(dst, src) if t == 1 else V.tensor_tensor(dst, src, dst, A.max), "exa")
-        wv("exa")
-        for o in (0, 32):
+                src = T.ps[64 * a:64 * a + 64, co + a:co + a + step * 7 + 1:step]
+                dst = T[to][0:64, h + a:h + B:2]
+                inc(V.tensor_copy(dst, src) if to == "e" else V.tensor_tensor(dst, src, T.e[0:64, h + a:h + B:2], A.max), sem)
+
+    def turn(to, fr, rows, sem):
+        for o in rows:
             for h in (0, 32):
-                inc(V.transpose(T.f[o:o + 32, h:h + 32], T.e[h:h + 32, 0:32]), "tr")
-        run = T.r[0:64, C * (t - 1):C * t]
-        ni = T.ni[0:64, t:t + 1]
-        wv("tr")
-        inc(V.tensor_tensor_scan(run, T.f[0:64, :], T.f[0:64, :], BIG, A.min, A.min), "scan")
+                inc(V.transpose(T[to][o:o + 32, h:h + 32], T[fr][h:h + 32, 0:32]), sem)
+
+    def local(t, at):
+        wv("pe")
+        if t == 1:
+            fold("e", 0, 514, "exa")
+        else:
+            fold("eb", 512, B + 2, "exa")
+        wv("exa")
+        turn("f", "e" if t == 1 else "eb", (0, 32), "tr")
+        run = T.r[lo, C * (t - 1):C * t]
+        ni = T.ni[lo, t:t + 1]
+        wv("pre", "tr")
+        if t == 1:
+            inc(V.tensor_tensor_scan(run, T.f[lo, :], T.f[lo, :], BIG, A.min, A.min), "scan")
+        else:
+            inc(V.tensor_tensor_scan(run, T.f[lo, :], T.dm[lo, :], sp(lo, t - 1, INIT), A.min, A.max), "scan")
         wsc("scan")
-        inc(S.activation(T.junk[0:64, :], run, AF.Sign, bias=T.r[0:64, mark(t)], scale=-1.0, accum_out=ni), "sgn")
-        wv("sgn")
+        inc(S.activation(T.junk[lo, :], run, AF.Sign, bias=T.r[lo, mark(t)], scale=-1.0, accum_out=ni), "sgn")
+        wv("prep", "sgn")
         for p in (0, 64):
-            inc(V.tensor_scalar(T.off[p:p + 64, 2 * t:2 * t + 1], ni, -1.0, T.bb[0:64, 1:2], A.mult, A.add), "lst")
-        wsc("sgn", "k3")
+            inc(V.tensor_scalar(T.off[p:p + 64, 2 * t:2 * t + 1], ni, -1.0 if t == 1 else sp(lo, t - 1, NEG),
+                                T.bb[lo, 1:2] if t == 1 else sp(lo, t - 1, B1), A.mult, A.add), "lst")
+        wsc("sgn", "k3", "prep")
+
+        def number(to):
+            inc(S.activation(to, T.ni[q0, t:t + 1], AF.Identity, bias=T.bb[q0, 2:3] if t == 1 else sp(q0, t - 1, B2),
+                             scale=-1.0 if t == 1 else sp(q0, t - 1, NEG)), "num")
         if t == R:
-            inc(S.activation(T.r[96:128, mark(t)], T.ni[0:32, t:t + 1], AF.Identity, bias=T.bb[0:32, 2:3], scale=-1.0), "num")
+            number(msg(top, t))
         wv("lst", "xq")
         inc(V.tensor_copy(wds("aq", at, at + B), wds("xq", 0, P).indirect(lst(t))), "pkc")
         wsc("lst", "xq")
         inc(S.activation(T.as_[:, at:at + B], T.xs[:, 0:P].indirect(lst(t)), AF.Copy), "pks")
         if t < R:
-            inc(S.activation(T.n1[64:128, t:t + 1], ni, AF.Identity, bias=T.bb[0:64, 2:3], scale=-1.0), "num")
+            number(T.n1[q0, t:t + 1])
 
     n = B * R
     n0 = n - B
+    LW = 16
+
+    def list_won(t):
+        for p in (lo, hi):
+            inc(V.tensor_scalar(T.off[p, 2 * LW + t - 1:2 * LW + t], T.sel[lo, 8 + t:9 + t], float(GAP),
+                                T.bb[lo, 3 + t:4 + t], A.mult, A.add), "lb")
+
     for t in range(1, R + 1):
         last = t == R
         c0 = 32 * (t - 1)
+        a0, b0 = at_a(t), at_b(t)
         col = slice(t, t + 1)
         sc = slice(8 + t, 9 + t)
-        mk = mark(t)
-        up = slice(64, 96 if last else 128)
-        sums = "w1" if t > 1 else "zr"
         if t == 1:
             wp("sq")
             for i, (a, b) in enumerate(CHUNKS):
@@ -146,119 +201,169 @@ def rank_program(g, core, T, topo):
                 inc(V.quantize_mx(T.xq[:, a:b], T.xs[:, a:b], T.xt[:, 4 * a:4 * b]), "xq")
                 wp("xq")
                 for k in range(a // 128, b // 128):
-                    score(k, "sq", "ss")
+                    product(k, k, "sq", "ss", 0, True, True, "pe")
         else:
-            wp("pbc", "pbs", "zq")
-            for k in range(8):
-                score(k, "hq", "hs")
+            wp("zq", "exa")
+            PE.wait_ge(T.sem["c2_%d" % (t - 1)], arrive_cross)
+            PE.wait_ge(T.sem["s2_%d" % (t - 1)], arrive_cross)
+            scores(1, at_b(t - 1), "pe")
         local(t, c0)
 
-        wg("scan", sums, *(["num"] if last else []))
-        send(mate, T.rx1[:, col], T.r[:, mk], "m1_%d" % t)
+        wg("zr", "pre", "scan", *(["num"] if last else []))
+        send(mate, T.rx1[:, col], msg(al, t), "m1_%d" % t)
         wg("pkc")
         send(mate, cds("aq", c0 + B, c0 + 2 * B), cds("aq", c0, c0 + B), "c1_%d" % t)
         wg("pks")
         send(mate, T.as_[:, c0 + B:c0 + 2 * B], T.as_[:, c0:c0 + B], "s1_%d" % t)
 
         if t == 1:
-            inc(V.quantize_mx(T.hq[:], T.hs[:], T.st[:]), "zq")
-            inc(V.memset(T.nn[:], 0.0), "zf")
-        if t == 2:
+            zeros(at_b(1) + B, at_a(2) + B)
+        if t in (2, 3):
+            zeros(at_a(t + 1) + B, at_b(t + 1) + B)
+        if t == 4:
             wv("w")
             inc(V.quantize_mx(T.wq[:], T.ws[:], T.wt[:]), "wq")
+        if 1 < t < R:
+            wsc("tr", "tra", "ga")
+            inc(S.activation(T.g1[q0, :], T.f[q0, :], AF.Copy, scale=T.sel[q0, 7 + t:8 + t]), "gs")
+            inc(S.activation(T.g2[q0, :], T.fa[q0, :], AF.Copy, scale=sp(q0, t - 1, NS)), "gs")
         if last:
-            wp("wq", "exa")
+            list_won(t - 1)
+            wv("lb", "zq", "pac")
+            inc(V.tensor_copy(wds("hq", 0, n0), wds("bq", 0, a0).indirect(lst(LW, R - 1))), "pbc")
+            wsc("lb", "zq", "pas")
+            inc(S.activation(T.hs[:, 0:n0], T.bs[:, 0:a0].indirect(lst(LW, R - 1)), AF.Copy), "pbt")
+            wp("wq", "pbc", "pbt")
             for o in range(O):
-                inc(PE.matmul_mx(T.ps[:, 512 * o:512 * o + 128], T.wq[:, 128 * o:128 * o + 128],
+                inc(PE.matmul_mx(T.ps[:, 1024 + 512 * o:1024 + 512 * o + 128], T.wq[:, 128 * o:128 * o + 128],
                                  T.ws[:, 128 * o:128 * o + 128], T.hq[:], T.hs[:], True, True), "pw")
-            wv("pw")
-            for o in range(O):
-                inc(V.tensor_copy(T.yo[:, n * o:n * o + n0], T.ps[:, 512 * o:512 * o + n0]), "yv")
-            wy("pbc", "pbs")
+            wy("pbc", "pbt")
             inc(SY.dma_start(T.oc[:, 0:4 * n0], cds("hq", 0, n0)), "dsy", 16)
             for k in range(4):
                 inc(SY.dma_start(T.osc[4 * k:4 * k + 4, 0:n0], T.hs[32 * k:32 * k + 4, 0:n0]), "dsy", 16)
-            wy("yv")
-            for o in range(O):
-                inc(SY.dma_start(T.y[:, n * o:n * o + n0], T.yo[:, n * o:n * o + n0]), "dsy", 16)
 
         V.wait_ge(T.sem["m1_%d" % t], arrive_mate)
         less = A.is_lt if rank & 1 == 0 else A.is_le
-        inc(V.tensor_scalar(T.sel[64:128, col], T.rx1[0:64, col], T.r[0:64, mk], None, less), "sela")
-        inc(V.tensor_scalar(T.sel[0:64, col], T.rx1[0:64, col], T.r[0:64, mk], None, less), "sela")
-        inc(V.tensor_tensor(T.tx2[0:64, col], T.rx1[0:64, col], T.r[0:64, mk], A.min), "t2")
+        inc(V.tensor_scalar(T.sel[hi, col], T.rx1[lo, col], msg(lo, t), None, less), "sela")
+        inc(V.tensor_scalar(T.sel[lo, col], T.rx1[lo, col], msg(lo, t), None, less), "sela")
+        inc(V.tensor_tensor(T.tx2[lo, col], T.rx1[lo, col], msg(lo, t), A.min), "t2")
         wv("sela")
         inc(V.tensor_scalar(lst(8 + t), T.sel[:, col], float(B), T.bb[:, 0:1], A.mult, A.add), "la")
-        wsc("num", sums)
+        wsc("num", "zr", "pre")
         S.wait_ge(T.sem["m1_%d" % t], arrive_mate)
         if last:
-            inc(S.activation(T.dd[96:128, col], T.r[96:128, mk], AF.Identity, bias=T.rx1[96:128, col], scale=-1.0), "da")
-        inc(S.activation(T.tx2[up, col], T.rx1[up, col], AF.Identity, bias=T.r[up, mk]), "n2")
+            inc(S.activation(T.dd[top, col], msg(top, t), AF.Identity, bias=T.rx1[top, col], scale=-1.0), "da")
+        inc(S.activation(T.tx2[up, col], T.rx1[up, col], AF.Identity, bias=msg(up, t)), "n2")
         if last:
             wsc("da", "sela")
-            inc(S.activation(T.tx2[96:128, col], T.dd[96:128, col], AF.Identity, bias=T.r[96:128, mk],
-                             scale=T.sel[96:128, col]), "n2")
+            inc(S.activation(T.tx2[top, col], T.dd[top, col], AF.Identity, bias=msg(top, t), scale=T.sel[top, col]), "n2")
+        else:
+            wsc("sela")
+            inc(S.activation(sp(q0, t, NS1), T.sel[q0, col], AF.Identity, bias=1.0, scale=-1.0), "ns1")
+            wsc("ns1")
+            inc(S.activation(sp(q0, t, X1), T.n1[q0, col], AF.Copy, scale=sp(q0, t, NS1)), "xn")
         wg("t2", "n2")
         send(cross, T.rx2[:, col], T.tx2[:, col], "m2_%d" % t)
         wv("la", "pkc")
         V.wait_ge(T.sem["c1_%d" % t], arrive_mate)
-        inc(V.tensor_copy(wds("bq", c0, c0 + B), wds("aq", c0, c0 + 2 * B).indirect(lst(8 + t))), "pac")
+        inc(V.tensor_copy(wds("bq", a0, a0 + B), wds("aq", c0, c0 + 2 * B).indirect(lst(8 + t))), "pac")
         wv("pks")
         V.wait_ge(T.sem["s1_%d" % t], arrive_mate)
-        inc(V.tensor_copy(T.bs[:, c0:c0 + B], T.as_[:, c0:c0 + 2 * B].indirect(lst(8 + t))), "pas")
+        inc(V.tensor_copy(T.bs[:, a0:a0 + B], T.as_[:, c0:c0 + 2 * B].indirect(lst(8 + t))), "pas")
 
         wg("pac")
-        send(cross, cds("bq", c0 + B, c0 + 2 * B), cds("bq", c0, c0 + B), "c2_%d" % t)
+        send(cross, cds("bq", b0, b0 + B), cds("bq", a0, a0 + B), "c2_%d" % t)
         wg("pas")
-        send(cross, T.bs[:, c0 + B:c0 + 2 * B], T.bs[:, c0:c0 + B], "s2_%d" % t)
+        send(cross, T.bs[:, b0:b0 + B], T.bs[:, a0:a0 + B], "s2_%d" % t)
+
+        if not last:
+            wp("zq", "exa", "exb", "pac", "pas")
+            scores(0, a0, "pea")
+            if t == 1:
+                zeros(at_b(2) + B)
+                inc(V.quantize_mx(T.hq[:], T.hs[:], T.st[:, 64:576]), "zq")
+            else:
+                wv("gs", "te")
+                inc(V.tensor_tensor(T.g3[q0, :], T.g1[q0, :], T.g2[q0, :], A.add), "ga")
+                list_won(t - 1)
+                wv("ga")
+                for h in (0, 32):
+                    inc(V.transpose(T.e[h:h + 32, 0:32], T.g3[q0, h:h + 32]), "te")
+            wv("te", "tra", "pea")
+            fold("ea", 0, B + 2, "exb")
+        else:
+            wv("pw")
+            for o in range(O):
+                inc(V.tensor_copy(T.yo[:, n * o:n * o + n0], T.ps[:, 1024 + 512 * o:1024 + 512 * o + n0]), "yv")
+            wy("yv")
+            for o in range(O):
+                inc(SY.dma_start(T.y[:, n * o:n * o + n0], T.yo[:, n * o:n * o + n0]), "dsy", 16)
 
         wv("t2")
         V.wait_ge(T.sem["m2_%d" % t], arrive_cross)
-        less = A.is_lt if rank & 2 == 0 else A.is_le
-        inc(V.tensor_scalar(T.sel[0:64, sc], T.rx2[0:64, col], T.tx2[0:64, col], None, less), "selb")
-        inc(V.tensor_scalar(T.sel[64:128, sc], T.rx2[0:64, col], T.tx2[0:64, col], None, less), "selb")
-        wv("selb")
-        inc(V.tensor_scalar(lst(16 + t), T.sel[:, sc], float(B), T.bb[:, 0:1], A.mult, A.add), "lb")
+        less, other = (A.is_lt, A.is_ge) if rank & 2 == 0 else (A.is_le, A.is_gt)
+        inc(V.tensor_scalar(T.sel[lo, sc], T.rx2[lo, col], T.tx2[lo, col], None, less), "selb")
+        if last:
+            inc(V.tensor_scalar(T.sel[hi, sc], T.rx2[lo, col], T.tx2[lo, col], None, less), "selb")
+            wv("selb")
+            inc(V.tensor_scalar(lst(24), T.sel[:, sc], float(B), T.bb[:, 0:1], A.mult, A.add), "lb")
+        else:
+            inc(V.tensor_scalar(sp(q0, t, NS), T.rx2[q0, col], T.tx2[q0, col], None, other), "selb")
+            wv("exb", "gs")
+            turn("fa", "ea", (0,), "tra")
+            wv("tra", "selb")
+            runa = T.ra[q0, C * t:C * t + C]
+            inc(V.tensor_tensor_scan(runa, T.fa[q0, :], T.fa[q0, :], BIG, A.min, A.min), "scana")
+            wsc("zf", "xn", "selb")
+            inc(S.activation(sp(lo, t, NEG, 2), T.kk[lo, :], AF.Copy, scale=T.sel[lo, sc]), "fac")
+            inc(S.activation(sp(lo, t, INIT), T.sel[lo, sc], AF.Identity, bias=T.kk[lo, 1:2], scale=2 * BIG), "pre")
+            inc(S.activation(msg(up, t + 1), sp(q0, t, X1), AF.Copy, scale=sp(q0, t, NS)), "pre")
+            inc(S.activation(sp(q0, t, NNS), sp(q0, t, NS), AF.Copy, scale=-1.0), "fac")
+            wsc("fac", "scana")
+            for q in (q0, q1):
+                inc(S.activation(T.dm[q, C - 1:C], T.ra[q0, mark(t + 1)], AF.Identity, bias=sp(q0, t, NB), scale=sp(q0, t, NS)), "pre")
+            inc(S.activation(T.junk[q0, :], runa, AF.Sign, bias=T.ra[q0, mark(t + 1)], scale=-1.0,
+                             accum_out=T.nia[q0, col]), "sgna")
+            wsc("sgna")
+            for q in (q0, q1):
+                inc(S.activation(sp(q, t, B1), T.nia[q0, col], AF.Identity, bias=T.bb[q0, 1:2], scale=sp(q0, t, NNS)), "prep")
+            inc(S.activation(sp(q0, t, B2), T.nia[q0, col], AF.Identity, bias=T.bb[q0, 2:3], scale=sp(q0, t, NNS)), "prep")
         if t > 1:
             wsc("n2", "zf")
             S.wait_ge(T.sem["m2_%d" % t], arrive_cross)
             if last:
-                inc(S.activation(T.dd[96:128, sc], T.tx2[96:128, col], AF.Identity, bias=T.rx2[96:128, col], scale=-1.0), "db")
-            inc(S.activation(T.nn[96:128, t - 2:t - 1], T.rx2[64:96, col], AF.Identity, bias=T.tx2[64:96, col]), "nn")
+                inc(S.activation(T.dd[top, sc], T.tx2[top, col], AF.Identity, bias=T.rx2[top, col], scale=-1.0), "db")
+            inc(S.activation(T.nn[top, t - 2:t - 1], T.rx2[up, col], AF.Identity, bias=T.tx2[up, col]), "nn")
             if last:
                 wsc("db", "selb")
-                inc(S.activation(T.nn[96:128, t - 1:t], T.dd[96:128, sc], AF.Identity, bias=T.tx2[96:128, col],
-                                 scale=T.sel[96:128, sc]), "nn")
-        h0 = B * (t - 1)
-        wv("lb", "pac", "zq")
-        V.wait_ge(T.sem["c2_%d" % t], arrive_cross)
-        inc(V.tensor_copy(wds("hq", h0, h0 + B), wds("bq", c0, c0 + 2 * B).indirect(lst(16 + t))), "pbc")
-        wv("pas")
-        V.wait_ge(T.sem["s2_%d" % t], arrive_cross)
-        inc(V.tensor_copy(T.hs[:, h0:h0 + B], T.bs[:, c0:c0 + 2 * B].indirect(lst(16 + t))), "pbs")
-        if not last:
-            inc(V.tensor_tensor(T.dd[64:128, sc], T.sel[64:128, col], T.sel[64:128, sc], A.add), "ws2")
-            wv("ws2", "num")
-            nxt = slice(64, 96 if t + 1 == R else 128)
-            inc(V.tensor_scalar(T.r[nxt, mark(t + 1)], T.dd[nxt, sc], 0.0, T.n1[nxt, col], A.is_equal, A.mult), "w1")
+                inc(S.activation(T.nn[top, t - 1:t], T.dd[top, sc], AF.Identity, bias=T.tx2[top, col],
+                                 scale=T.sel[top, sc]), "nn")
 
+    wv("lb", "pac", "pw")
+    V.wait_ge(T.sem["c2_%d" % R], arrive_cross)
+    inc(V.tensor_copy(wds("hq", n0, n), wds("bq", a0, a0 + 2 * B).indirect(lst(24))), "pbc")
+    wv("pas")
+    V.wait_ge(T.sem["s2_%d" % R], arrive_cross)
+    inc(V.tensor_copy(T.hs[:, n0:n], T.bs[:, a0:a0 + 2 * B].indirect(lst(24))), "pbs")
     wp("pbc", "pbs")
     for o in range(O):
-        inc(PE.matmul_mx(T.ps[:, 1024 + 512 * o:1024 + 512 * o + 128], T.wq[:, 128 * o:128 * o + 128],
+        inc(PE.matmul_mx(T.ps[:, 2048 + 512 * o:2048 + 512 * o + 128], T.wq[:, 128 * o:128 * o + 128],
                          T.ws[:, 128 * o:128 * o + 128], T.hq[:], T.hs[:], True, True), "py%d" % o)
     wy("pbc")
     inc(SY.dma_start(T.oc[:, 4 * n0:4 * n], cds("hq", n0, n)), "dsy", 16)
     wsc("pbs")
+    wy("pbs")
     for k in range(4):
-        inc(S.dma_start(T.osc[4 * k:4 * k + 4, n0:n], T.hs[32 * k:32 * k + 4, n0:n]), "dsc", 16)
+        q, s = ((S, "dsc"), (SY, "dsy"))[k % 2]
+        inc(q.dma_start(T.osc[4 * k:4 * k + 4, n0:n], T.hs[32 * k:32 * k + 4, n0:n]), s, 16)
     wv("nn")
     inc(V.transpose(T.nt[96:128, :], T.nn[96:128, :]), "ntr")
-    wy("ntr")
-    inc(SY.dma_start(T.nb[:], T.nt[96:96 + R, 0:B]), "dsy", 16)
+    wsc("ntr")
+    inc(S.dma_start(T.nb[:], T.nt[96:96 + R, 0:B]), "dsc", 16)
     wv("py0")
-    inc(V.tensor_copy(T.yl[:, 0:B], T.ps[:, 1024 + n0:1024 + n]), "yl0")
+    inc(V.tensor_copy(T.yl[:, 0:B], T.ps[:, 2048 + n0:2048 + n]), "yl0")
     wsc("py1")
-    inc(S.activation(T.yl[:, B:2 * B], T.ps[:, 1536 + n0:1536 + n], AF.Copy), "yl1")
+    inc(S.activation(T.yl[:, B:2 * B], T.ps[:, 2560 + n0:2560 + n], AF.Copy), "yl1")
     wy("yl0")
     inc(SY.dma_start(T.y[:, n0:n], T.yl[:, 0:B]), "dsy", 16)
     wsc("yl1")

from concourse.mybir import dt, AluOpType, ActivationFunctionType

N, P, R, O = 4, 1024, 5, 2
B = 16
C = P // B
BIG = 2.0 ** 98
F8, U8, F32, BF, I32, U16 = "float8_e4m3fn_x4", "uint8", "float32", "bfloat16", "int32", "uint16"
CHUNKS = [(0, 256), (256, 640), (640, 896), (896, 1024)]
Z = 128
GAP = B + Z
WB = Z + 2 * GAP * (R - 1) + 2 * B

SCRATCH = {
    "xt": ("sbuf", [128, 4 * P], BF), "xq": ("sbuf", [128, P], F8), "xs": ("sbuf", [128, P], U8),
    "st": ("sbuf", [128, 576], BF),
    "wt": ("sbuf", [128, 512 * O], BF), "wq": ("sbuf", [128, 128 * O], F8), "ws": ("sbuf", [128, 128 * O], U8),
    "sq": ("sbuf", [128, 128], F8), "ss": ("sbuf", [128, 128], U8),
    "aq": ("sbuf", [128, 192], F8), "as_": ("sbuf", [128, 192], U8),
    "bq": ("sbuf", [128, WB], F8), "bs": ("sbuf", [128, WB], U8),
    "hq": ("sbuf", [128, 128], F8), "hs": ("sbuf", [128, 128], U8),
    "e": ("sbuf", [128, 32], F32), "ea": ("sbuf", [128, 32], F32), "eb": ("sbuf", [128, 32], F32),
    "f": ("sbuf", [128, 64], F32), "fa": ("sbuf", [128, 64], F32), "dm": ("sbuf", [128, 64], F32),
    "g1": ("sbuf", [128, 64], F32), "g2": ("sbuf", [128, 64], F32), "g3": ("sbuf", [128, 64], F32),
    "r": ("sbuf", [128, 64 * R], F32), "ra": ("sbuf", [128, 64 * R], F32),
    "junk": ("sbuf", [128, 64], F32), "ni": ("sbuf", [128, 8], F32), "nia": ("sbuf", [128, 8], F32),
    "sp": ("sbuf", [128, 16 * R], F32), "kk": ("sbuf", [128, 2], F32),
    "rx1": ("sbuf", [128, 8], F32), "tx2": ("sbuf", [128, 8], F32), "rx2": ("sbuf", [128, 8], F32),
    "sel": ("sbuf", [128, 16], F32), "dd": ("sbuf", [128, 16], F32), "n1": ("sbuf", [128, 8], F32),
    "off": ("sbuf", [128, 64], U16),
    "ip": ("sbuf", [128, 4], I32), "ia": ("sbuf", [128, 8], F32),
    "bb": ("sbuf", [128, 12], F32),
    "nn": ("sbuf", [128, 32], F32), "nt": ("sbuf", [128, 32], F32),
    "yo": ("sbuf", [128, 80 * O], F32), "yl": ("sbuf", [128, B * O], F32),
    "ps": ("psum", [128, 4096], F32),
}
_LOCAL = ["sz", "zf", "zr", "io1", "io2", "k1", "k2", "k3", "seed", "sq", "w", "wq", "x0", "x1", "x2", "x3", "zq",
          "xq", "pe", "exa", "tr", "scan", "sgn", "num", "lst", "pkc", "pks",
          "pea", "exb", "tra", "scana", "sgna", "fac", "pre", "prep", "ns1", "xn", "gs", "ga", "te",
          "sela", "la", "t2", "n2", "da", "pac", "pas", "selb", "lb", "db", "nn", "pbc", "pbs", "pbt",
          "pw", "py0", "py1", "yv", "yl0", "yl1", "ntr", "dsy", "dsc", "sent"]
_ARRIVE = ["%s%d_%d" % (k, h, t) for k in "csm" for h in (1, 2) for t in range(1, R + 1)]
SEMAPHORES = _LOCAL + _ARRIVE


def rank_program(g, core, T, topo):
    rank = T.rank_of(core)
    if rank is None:
        return
    V, S, PE, SY = g.vector, g.scalar, g.tensor, g.sync
    A, AF = AluOpType, ActivationFunctionType
    tot, seen = {}, {}

    def inc(ins, s, n=1):
        ins.then_inc(T.sem[s], n)
        tot[s] = tot.get(s, 0) + n

    def w(q, name, *sems):
        for s in sems:
            if seen.get((name, s), 0) < tot.get(s, 0):
                q.wait_ge(T.sem[s], tot[s])
                seen[(name, s)] = tot[s]
                seen[s] = max(seen.get(s, 0), tot[s])

    def wv(*s): w(V, "v", *s)
    def wsc(*s): w(S, "s", *s)
    def wp(*s): w(PE, "p", *s)
    def wg(*s): w(g, "g", *s)
    def wy(*s): w(SY, "y", *s)

    def cds(name, a, b): return T[name][:, a:b].bitcast(dt.uint8)
    def wds(name, a, b): return T[name][:, a:b].bitcast(dt.uint32)
    def lst(i, k=1): return T.off[:, 2 * i:2 * i + k]

    def send(peer, dst, src, arrive):
        rid, pid, _ = topo.addr(peer)
        g.remote_dma(dst, src, T.sem[arrive], T.sem.sent, pid, rid, topo.mask(core, peer))
        tot["sent"] = tot.get("sent", 0) + len(topo.engines(core, peer))

    mate = T.cores[rank ^ 1]
    cross = T.cores[rank ^ 2]
    arrive_mate = len(topo.engines(mate, core))
    arrive_cross = len(topo.engines(cross, core))

    def at_a(t): return Z + 2 * GAP * (t - 1)
    def at_b(t): return at_a(t) + (GAP if t < R else B)

    def zeros(*cols):
        for c in cols:
            inc(V.quantize_mx(T.bq[:, c:c + Z], T.bs[:, c:c + Z], T.st[:, 64:576]), "zq")

    lo, hi, al = slice(0, 64), slice(64, 128), slice(0, 128)
    q0, q1, up, top = slice(0, 32), slice(32, 64), slice(64, 96), slice(96, 128)

    inc(S.dma_start(T.st[:, 0:64], T.seed[:]), "seed", 16)
    for i, (a, b) in enumerate(CHUNKS):
        q = (SY, S)[i % 2]
        inc(q.dma_start(T.xt[:, 4 * a:4 * b], T.x[:, 4 * a:4 * b]), "x%d" % i, 16)
    inc(S.dma_start(T.wt[:], T.w[:]), "w", 16)

    inc(g.iota(T.ip[:, 0:1], [[0, 1]], 0, 1), "io1")
    inc(g.iota(T.ia[:, 0:R - 1], [[2 * GAP, R - 1]], Z, 0, allow_small_or_imprecise_dtypes=True), "io2")
    inc(V.memset(T.st[:, 64:576], 0.0), "sz")
    inc(V.memset(T.r[hi, C - 1:C * R:C], 0.0), "zr")
    inc(V.memset(T.tx2[top, :], 0.0), "zr")
    wv("io1")
    inc(V.tensor_scalar(T.ip[:, 2:3], T.ip[:, 0:1], B - 1, None, A.bitwise_and), "k1")
    inc(V.memset(T.nn[:], 0.0), "zf")
    wv("k1")
    inc(V.tensor_copy(T.bb[:, 0:1], T.ip[:, 2:3]), "k2")
    inc(V.memset(T.dm[lo, :], -BIG), "zf")
    wv("k2", "io2")
    inc(V.tensor_scalar(T.bb[:, 1:2], T.bb[:, 0:1], float(C), None, A.mult), "k3")
    inc(V.tensor_scalar(T.bb[:, 2:3], T.bb[:, 0:1], float(C), float(P * rank), A.mult, A.add), "k3")
    inc(V.tensor_scalar(T.bb[:, 4:3 + R], T.ia[:, 0:R - 1], T.bb[:, 0:1], None, A.add), "k3")
    inc(V.memset(T.kk[lo, 0:1], -1.0), "zf")
    inc(V.memset(T.kk[lo, 1:2], -BIG), "zf")
    wv("sz")
    zeros(0, at_a(1) + B)
    wv("seed", "k3")
    inc(V.quantize_mx(T.sq[:], T.ss[:], T.st[:, 0:512]), "sq")

    def product(bank, k, mq, ms, c, first, final, sem):
        inc(PE.matmul_mx(T.ps[:, 512 * bank:512 * bank + 128], T.xq[:, 128 * k:128 * k + 128], T.xs[:, 128 * k:128 * k + 128],
                         T[mq][:, c:c + 128], T[ms][:, c:c + 128], first, final), sem)

    def scores(bank, c, sem):
        for k in range(8):
            product(bank, k, "bq", "bs", c - B * k, k == 0, k == 7, sem)

    def mark(t): return slice(C * t - 1, C * t)
    def msg(rows, t): return T.r[rows, mark(t)]
    def sp(rows, t, i, k=1): return T.sp[rows, 16 * t + i:16 * t + i + k]
    NS, NEG, NB, NNS, INIT, B1, B2, X1, NS1 = range(9)

    def fold(to, co, step, sem):
        for h in (0, B):
            for a in (0, 1):
                src = T.ps[64 * a:64 * a + 64, co + a:co + a + step * 7 + 1:step]
                dst = T[to][0:64, h + a:h + B:2]
                inc(V.tensor_copy(dst, src) if to == "e" else V.tensor_tensor(dst, src, T.e[0:64, h + a:h + B:2], A.max), sem)

    def turn(to, fr, rows, sem):
        for o in rows:
            for h in (0, 32):
                inc(V.transpose(T[to][o:o + 32, h:h + 32], T[fr][h:h + 32, 0:32]), sem)

    def local(t, at):
        wv("pe")
        if t == 1:
            fold("e", 0, 514, "exa")
        else:
            fold("eb", 512, B + 2, "exa")
        wv("exa")
        turn("f", "e" if t == 1 else "eb", (0, 32), "tr")
        run = T.r[lo, C * (t - 1):C * t]
        ni = T.ni[lo, t:t + 1]
        wv("pre", "tr")
        if t == 1:
            inc(V.tensor_tensor_scan(run, T.f[lo, :], T.f[lo, :], BIG, A.min, A.min), "scan")
        else:
            inc(V.tensor_tensor_scan(run, T.f[lo, :], T.dm[lo, :], sp(lo, t - 1, INIT), A.min, A.max), "scan")
        wsc("scan")
        inc(S.activation(T.junk[lo, :], run, AF.Sign, bias=T.r[lo, mark(t)], scale=-1.0, accum_out=ni), "sgn")
        wv("prep", "sgn")
        for p in (0, 64):
            inc(V.tensor_scalar(T.off[p:p + 64, 2 * t:2 * t + 1], ni, -1.0 if t == 1 else sp(lo, t - 1, NEG),
                                T.bb[lo, 1:2] if t == 1 else sp(lo, t - 1, B1), A.mult, A.add), "lst")
        wsc("sgn", "k3", "prep")

        def number(to):
            inc(S.activation(to, T.ni[q0, t:t + 1], AF.Identity, bias=T.bb[q0, 2:3] if t == 1 else sp(q0, t - 1, B2),
                             scale=-1.0 if t == 1 else sp(q0, t - 1, NEG)), "num")
        if t == R:
            number(msg(top, t))
        wv("lst", "xq")
        inc(V.tensor_copy(wds("aq", at, at + B), wds("xq", 0, P).indirect(lst(t))), "pkc")
        wsc("lst", "xq")
        inc(S.activation(T.as_[:, at:at + B], T.xs[:, 0:P].indirect(lst(t)), AF.Copy), "pks")
        if t < R:
            number(T.n1[q0, t:t + 1])

    n = B * R
    n0 = n - B
    LW = 16

    def list_won(t):
        for p in (lo, hi):
            inc(V.tensor_scalar(T.off[p, 2 * LW + t - 1:2 * LW + t], T.sel[lo, 8 + t:9 + t], float(GAP),
                                T.bb[lo, 3 + t:4 + t], A.mult, A.add), "lb")

    for t in range(1, R + 1):
        last = t == R
        c0 = 32 * (t - 1)
        a0, b0 = at_a(t), at_b(t)
        col = slice(t, t + 1)
        sc = slice(8 + t, 9 + t)
        if t == 1:
            wp("sq")
            for i, (a, b) in enumerate(CHUNKS):
                wv("x%d" % i)
                inc(V.quantize_mx(T.xq[:, a:b], T.xs[:, a:b], T.xt[:, 4 * a:4 * b]), "xq")
                wp("xq")
                for k in range(a // 128, b // 128):
                    product(k, k, "sq", "ss", 0, True, True, "pe")
        else:
            wp("zq", "exa")
            PE.wait_ge(T.sem["c2_%d" % (t - 1)], arrive_cross)
            PE.wait_ge(T.sem["s2_%d" % (t - 1)], arrive_cross)
            scores(1, at_b(t - 1), "pe")
        local(t, c0)

        wg("zr", "pre", "scan", *(["num"] if last else []))
        send(mate, T.rx1[:, col], msg(al, t), "m1_%d" % t)
        wg("pkc")
        send(mate, cds("aq", c0 + B, c0 + 2 * B), cds("aq", c0, c0 + B), "c1_%d" % t)
        wg("pks")
        send(mate, T.as_[:, c0 + B:c0 + 2 * B], T.as_[:, c0:c0 + B], "s1_%d" % t)

        if t == 1:
            zeros(at_b(1) + B, at_a(2) + B)
        if t in (2, 3):
            zeros(at_a(t + 1) + B, at_b(t + 1) + B)
        if t == 4:
            wv("w")
            inc(V.quantize_mx(T.wq[:], T.ws[:], T.wt[:]), "wq")
        if 1 < t < R:
            wsc("tr", "tra", "ga")
            inc(S.activation(T.g1[q0, :], T.f[q0, :], AF.Copy, scale=T.sel[q0, 7 + t:8 + t]), "gs")
            inc(S.activation(T.g2[q0, :], T.fa[q0, :], AF.Copy, scale=sp(q0, t - 1, NS)), "gs")
        if last:
            list_won(t - 1)
            wv("lb", "zq", "pac")
            inc(V.tensor_copy(wds("hq", 0, n0), wds("bq", 0, a0).indirect(lst(LW, R - 1))), "pbc")
            wsc("lb", "zq", "pas")
            inc(S.activation(T.hs[:, 0:n0], T.bs[:, 0:a0].indirect(lst(LW, R - 1)), AF.Copy), "pbt")
            wp("wq", "pbc", "pbt")
            for o in range(O):
                inc(PE.matmul_mx(T.ps[:, 1024 + 512 * o:1024 + 512 * o + 128], T.wq[:, 128 * o:128 * o + 128],
                                 T.ws[:, 128 * o:128 * o + 128], T.hq[:], T.hs[:], True, True), "pw")
            wy("pbc", "pbt")
            inc(SY.dma_start(T.oc[:, 0:4 * n0], cds("hq", 0, n0)), "dsy", 16)
            for k in range(4):
                inc(SY.dma_start(T.osc[4 * k:4 * k + 4, 0:n0], T.hs[32 * k:32 * k + 4, 0:n0]), "dsy", 16)

        V.wait_ge(T.sem["m1_%d" % t], arrive_mate)
        less = A.is_lt if rank & 1 == 0 else A.is_le
        inc(V.tensor_scalar(T.sel[hi, col], T.rx1[lo, col], msg(lo, t), None, less), "sela")
        inc(V.tensor_scalar(T.sel[lo, col], T.rx1[lo, col], msg(lo, t), None, less), "sela")
        inc(V.tensor_tensor(T.tx2[lo, col], T.rx1[lo, col], msg(lo, t), A.min), "t2")
        wv("sela")
        inc(V.tensor_scalar(lst(8 + t), T.sel[:, col], float(B), T.bb[:, 0:1], A.mult, A.add), "la")
        wsc("num", "zr", "pre")
        S.wait_ge(T.sem["m1_%d" % t], arrive_mate)
        if last:
            inc(S.activation(T.dd[top, col], msg(top, t), AF.Identity, bias=T.rx1[top, col], scale=-1.0), "da")
        inc(S.activation(T.tx2[up, col], T.rx1[up, col], AF.Identity, bias=msg(up, t)), "n2")
        if last:
            wsc("da", "sela")
            inc(S.activation(T.tx2[top, col], T.dd[top, col], AF.Identity, bias=msg(top, t), scale=T.sel[top, col]), "n2")
        else:
            wsc("sela")
            inc(S.activation(sp(q0, t, NS1), T.sel[q0, col], AF.Identity, bias=1.0, scale=-1.0), "ns1")
            wsc("ns1")
            inc(S.activation(sp(q0, t, X1), T.n1[q0, col], AF.Copy, scale=sp(q0, t, NS1)), "xn")
        wg("t2", "n2")
        send(cross, T.rx2[:, col], T.tx2[:, col], "m2_%d" % t)
        wv("la", "pkc")
        V.wait_ge(T.sem["c1_%d" % t], arrive_mate)
        inc(V.tensor_copy(wds("bq", a0, a0 + B), wds("aq", c0, c0 + 2 * B).indirect(lst(8 + t))), "pac")
        wv("pks")
        V.wait_ge(T.sem["s1_%d" % t], arrive_mate)
        inc(V.tensor_copy(T.bs[:, a0:a0 + B], T.as_[:, c0:c0 + 2 * B].indirect(lst(8 + t))), "pas")

        wg("pac")
        send(cross, cds("bq", b0, b0 + B), cds("bq", a0, a0 + B), "c2_%d" % t)
        wg("pas")
        send(cross, T.bs[:, b0:b0 + B], T.bs[:, a0:a0 + B], "s2_%d" % t)

        if not last:
            wp("zq", "exa", "exb", "pac", "pas")
            scores(0, a0, "pea")
            if t == 1:
                zeros(at_b(2) + B)
                inc(V.quantize_mx(T.hq[:], T.hs[:], T.st[:, 64:576]), "zq")
            else:
                wv("gs", "te")
                inc(V.tensor_tensor(T.g3[q0, :], T.g1[q0, :], T.g2[q0, :], A.add), "ga")
                list_won(t - 1)
                wv("ga")
                for h in (0, 32):
                    inc(V.transpose(T.e[h:h + 32, 0:32], T.g3[q0, h:h + 32]), "te")
            wv("te", "tra", "pea")
            fold("ea", 0, B + 2, "exb")
        else:
            wv("pw")
            for o in range(O):
                inc(V.tensor_copy(T.yo[:, n * o:n * o + n0], T.ps[:, 1024 + 512 * o:1024 + 512 * o + n0]), "yv")
            wy("yv")
            for o in range(O):
                inc(SY.dma_start(T.y[:, n * o:n * o + n0], T.yo[:, n * o:n * o + n0]), "dsy", 16)

        wv("t2")
        V.wait_ge(T.sem["m2_%d" % t], arrive_cross)
        less, other = (A.is_lt, A.is_ge) if rank & 2 == 0 else (A.is_le, A.is_gt)
        inc(V.tensor_scalar(T.sel[lo, sc], T.rx2[lo, col], T.tx2[lo, col], None, less), "selb")
        if last:
            inc(V.tensor_scalar(T.sel[hi, sc], T.rx2[lo, col], T.tx2[lo, col], None, less), "selb")
            wv("selb")
            inc(V.tensor_scalar(lst(24), T.sel[:, sc], float(B), T.bb[:, 0:1], A.mult, A.add), "lb")
        else:
            inc(V.tensor_scalar(sp(q0, t, NS), T.rx2[q0, col], T.tx2[q0, col], None, other), "selb")
            wv("exb", "gs")
            turn("fa", "ea", (0,), "tra")
            wv("tra", "selb")
            runa = T.ra[q0, C * t:C * t + C]
            inc(V.tensor_tensor_scan(runa, T.fa[q0, :], T.fa[q0, :], BIG, A.min, A.min), "scana")
            wsc("zf", "xn", "selb")
            inc(S.activation(sp(lo, t, NEG, 2), T.kk[lo, :], AF.Copy, scale=T.sel[lo, sc]), "fac")
            inc(S.activation(sp(lo, t, INIT), T.sel[lo, sc], AF.Identity, bias=T.kk[lo, 1:2], scale=2 * BIG), "pre")
            inc(S.activation(msg(up, t + 1), sp(q0, t, X1), AF.Copy, scale=sp(q0, t, NS)), "pre")
            inc(S.activation(sp(q0, t, NNS), sp(q0, t, NS), AF.Copy, scale=-1.0), "fac")
            wsc("fac", "scana")
            for q in (q0, q1):
                inc(S.activation(T.dm[q, C - 1:C], T.ra[q0, mark(t + 1)], AF.Identity, bias=sp(q0, t, NB), scale=sp(q0, t, NS)), "pre")
            inc(S.activation(T.junk[q0, :], runa, AF.Sign, bias=T.ra[q0, mark(t + 1)], scale=-1.0,
                             accum_out=T.nia[q0, col]), "sgna")
            wsc("sgna")
            for q in (q0, q1):
                inc(S.activation(sp(q, t, B1), T.nia[q0, col], AF.Identity, bias=T.bb[q0, 1:2], scale=sp(q0, t, NNS)), "prep")
            inc(S.activation(sp(q0, t, B2), T.nia[q0, col], AF.Identity, bias=T.bb[q0, 2:3], scale=sp(q0, t, NNS)), "prep")
        if t > 1:
            wsc("n2", "zf")
            S.wait_ge(T.sem["m2_%d" % t], arrive_cross)
            if last:
                inc(S.activation(T.dd[top, sc], T.tx2[top, col], AF.Identity, bias=T.rx2[top, col], scale=-1.0), "db")
            inc(S.activation(T.nn[top, t - 2:t - 1], T.rx2[up, col], AF.Identity, bias=T.tx2[up, col]), "nn")
            if last:
                wsc("db", "selb")
                inc(S.activation(T.nn[top, t - 1:t], T.dd[top, sc], AF.Identity, bias=T.tx2[top, col],
                                 scale=T.sel[top, sc]), "nn")

    wv("lb", "pac", "pw")
    V.wait_ge(T.sem["c2_%d" % R], arrive_cross)
    inc(V.tensor_copy(wds("hq", n0, n), wds("bq", a0, a0 + 2 * B).indirect(lst(24))), "pbc")
    wv("pas")
    V.wait_ge(T.sem["s2_%d" % R], arrive_cross)
    inc(V.tensor_copy(T.hs[:, n0:n], T.bs[:, a0:a0 + 2 * B].indirect(lst(24))), "pbs")
    wp("pbc", "pbs")
    for o in range(O):
        inc(PE.matmul_mx(T.ps[:, 2048 + 512 * o:2048 + 512 * o + 128], T.wq[:, 128 * o:128 * o + 128],
                         T.ws[:, 128 * o:128 * o + 128], T.hq[:], T.hs[:], True, True), "py%d" % o)
    wy("pbc")
    inc(SY.dma_start(T.oc[:, 4 * n0:4 * n], cds("hq", n0, n)), "dsy", 16)
    wsc("pbs")
    wy("pbs")
    for k in range(4):
        q, s = ((S, "dsc"), (SY, "dsy"))[k % 2]
        inc(q.dma_start(T.osc[4 * k:4 * k + 4, n0:n], T.hs[32 * k:32 * k + 4, n0:n]), s, 16)
    wv("nn")
    inc(V.transpose(T.nt[96:128, :], T.nn[96:128, :]), "ntr")
    wsc("ntr")
    inc(S.dma_start(T.nb[:], T.nt[96:96 + R, 0:B]), "dsc", 16)
    wv("py0")
    inc(V.tensor_copy(T.yl[:, 0:B], T.ps[:, 2048 + n0:2048 + n]), "yl0")
    wsc("py1")
    inc(S.activation(T.yl[:, B:2 * B], T.ps[:, 2560 + n0:2560 + n], AF.Copy), "yl1")
    wy("yl0")
    inc(SY.dma_start(T.y[:, n0:n], T.yl[:, 0:B]), "dsy", 16)
    wsc("yl1")
    inc(S.dma_start(T.y[:, n + n0:2 * n], T.yl[:, B:2 * B]), "dsc", 16)
    for s in tot:
        if seen.get(s, 0) < tot[s]:
            wg(s)
